import numpy as np
import ml_dtypes


def mxq(x, axis, fmt="e4m3"):
    dtype, down = {"e4m3": (ml_dtypes.float8_e4m3fn, 7), "e5m2": (ml_dtypes.float8_e5m2, 14)}[fmt]
    v = np.moveaxis(np.asarray(x, np.float32).astype(ml_dtypes.bfloat16).astype(np.float64), axis, -1)
    blocks = v.reshape(v.shape[:-1] + (-1, 32))
    amax = np.abs(blocks).max(-1, keepdims=True)
    byte = np.maximum(np.where(amax > 0, np.frexp(amax)[1] - 1 + 127, 0) - down, 1)
    scale = np.exp2(byte - 127.0)
    codes = (blocks / scale).astype(np.float32).astype(dtype).astype(np.float64)
    return np.moveaxis((codes * scale).reshape(v.shape), -1, axis)


WIDE = False


def mx_kscale(k):
    if not WIDE:
        return np.ones(k)
    levels = np.array([10, -10, 5, -5, 0])
    if k % 512:
        return np.exp2(np.random.permutation(np.resize(levels, k // 32))).repeat(32)
    a = np.empty((k // 512, 16))
    for p in range(k // 512):
        a[p, :8] = np.random.permutation(np.resize(levels, 8))
        for g in range(8):
            far = levels[np.abs(levels - a[p, g]) >= 10]
            a[p, g + 8] = far[np.random.randint(len(far))]
    return np.exp2(a.ravel()).repeat(32)


def f64(x):
    return np.asarray(x).astype(np.float64)


def striped(idx):
    return np.tile(idx.reshape(-1, 16).T, (8, 1)).astype(np.uint16)


def unstriped(offs):
    return offs[:16].T.reshape(-1).astype(np.int64)


def striped8(idx):
    return np.concatenate([x.reshape(-1, 16).T for x in idx]).astype(np.uint16)


def runs(offs, k):
    lists = np.stack([offs[16 * r : 16 * r + 16].T.reshape(-1) for r in range(8)]).astype(np.int64)
    return lists[np.arange(k) % 512 // 64]


def pack_weight(w):
    k, n = w.shape
    w = f64(np.asarray(w, np.float32).astype(ml_dtypes.bfloat16)).reshape(k // 32, 32, n)
    amax = np.abs(w).max(1)
    byte = np.clip(np.where(amax > 0, np.frexp(amax)[1] - 1 + 127 - 7, 1), 1, 254)
    scaled = (w * np.exp2(127.0 - byte)[:, None, :]).reshape(k, n).astype(np.float32)
    words = np.ascontiguousarray(scaled.reshape(k // 512, 128, 4, n).transpose(0, 1, 3, 2)).astype(ml_dtypes.float8_e4m3fn).view(np.uint8)
    return words, np.ascontiguousarray(byte.astype(np.uint8).reshape(k // 512, 16, n))


def unpack_weight(words, scales):
    g, p, n, _ = words.shape
    vals = np.ascontiguousarray(words).view(ml_dtypes.float8_e4m3fn).astype(np.float64) * np.repeat(np.exp2(scales.astype(np.float64) - 127.0), 8, axis=1)[..., None]
    return vals.transpose(0, 1, 3, 2).reshape(g * 512, n)


def sigmoid(v):
    return 1.0 / (1.0 + np.exp(-np.maximum(v, -700.0)))


K, T, S, H, G = 512, 1024, 512, 512, 2048


def setup_inputs():
    n = np.random.standard_normal
    s = mx_kscale(K)[:, None]
    packed_xT = pack_weight(n((K, T)) * s)
    packed_dT = pack_weight(n((K, G)) / s)
    return {
        "x_words": packed_xT[0],
        "x_scales": packed_xT[1],
        "w1": (n((K, H)) / np.sqrt(K) / s).astype(np.float32),
        "w2": (n((K, H)) / np.sqrt(K) / s).astype(np.float32),
        "gs": (np.random.uniform(0.5, 1.5, (K, 1)) * s).astype(np.float32),
        "d_words": packed_dT[0],
        "d_scales": packed_dT[1],
        "offs": striped(np.random.permutation(T)[:S]),
        "two": striped(np.random.permutation(T)[:S]),
        "n1": striped8(np.stack([np.random.permutation(S) for _ in range(8)])),
        "n2": striped8(np.stack([np.random.permutation(S) for _ in range(8)])),
        "k1": striped8(np.random.randint(0, G, (8, H))),
        "n3": striped8(np.stack([np.random.permutation(S) for _ in range(8)])),
        "n4": striped8(np.stack([np.random.permutation(S) for _ in range(8)])),
    }


def reference(x_words, x_scales, w1, w2, gs, d_words, d_scales, offs, two, n1, n2, k1, n3, n4):
    d_k1 = unpack_weight(d_words, d_scales)[np.arange(K)[:, None], runs(k1, K)]
    xq = unpack_weight(x_words, x_scales)[:, unstriped(offs)]
    y = mxq(f64(w1), 0, "e4m3").T @ xq
    x_two = unpack_weight(x_words, x_scales)[:, unstriped(two)]
    d = mxq(f64(w2), 0, "e4m3").T @ x_two
    z = f64(gs) * ((y + y[np.arange(H)[:, None], runs(n1, H)]) * (sigmoid(d + d[np.arange(H)[:, None], runs(n2, H)])))
    h = 0.0625 * ((d_k1.T @ mxq(z, 0, "e4m3")))
    pa = h[np.arange(H)[:, None], runs(n3, H)]
    pb = h[np.arange(H)[:, None], runs(n4, H)]
    mu = 0.3125 * (h + pa + pb)
    return (h - mu) / (np.sqrt((pa - mu) ** 2 + (pb - mu) ** 2 + 0.25))

@@ -1,0 +1,272 @@
+import math
+from contextlib import ExitStack
+
+import concourse.mybir as mybir
+from concourse.masks import make_identity
+
+K, T, S, H, G = 512, 1024, 512, 512, 2048
+FLOPS = 3 * 2 * K * H * S
+
+F32 = mybir.dt.float32
+BF16 = mybir.dt.bfloat16
+I32 = mybir.dt.int32
+U32 = mybir.dt.uint32
+U16 = mybir.dt.uint16
+U8 = mybir.dt.uint8
+FP8X4 = mybir.dt.float8_e4m3fn_x4
+ALU = mybir.AluOpType
+ACT = mybir.ActivationFunctionType
+
+P = 128
+NT = 4
+FIRST = 384
+ALPHA = 8.0 / 55.0
+HS = 0.0625
+
+
+def tile_picked_twqtriebstd_none_p_kernel(
+    tc, x_words, x_scales, w1, w2, gs, d_words, d_scales, offs, two, n1, n2, k1, n3, n4, out
+):
+    nc = tc.nc
+    with ExitStack() as ctx:
+        lists = ctx.enter_context(tc.tile_pool(name="lists", bufs=1))
+        keep = ctx.enter_context(tc.tile_pool(name="keep", bufs=1))
+        psum = ctx.enter_context(tc.psum_pool(name="psum", bufs=1))
+
+        def sb(name, shape, dtype):
+            return keep.tile(shape, dtype, name=name, align_bytes=64)
+
+        def bank(b, name):
+            return psum.tile([P, 512], F32, name=name, tag="bank%d" % b)
+
+        def load_list(name, src):
+            tile = lists.tile([P, S // 16], U16, name=name)
+            nc.sync.dma_start(tile[:], src)
+            return tile
+
+        def add_transpose(dst, src, start, stop):
+            nc.tensor.matmul(dst, src, ident[:], start=start, stop=stop, is_transpose=True)
+
+        xs_win = sb("xs_win", [P, T], U8)
+        ds_win = sb("ds_win", [P, G], U8)
+        ds_plane = sb("ds_plane", [P, H], U8)
+        nc.vector.memset(xs_win[:].bitcast(I32), 0)
+        nc.vector.memset(ds_win[:].bitcast(I32), 0)
+        warm = sb("warm", [P, 2], F32)
+        nc.vector.memset(warm[:, 0:1], 0.0)
+        nc.scalar.activation(warm[:, 1:2], warm[:, 0:1], ACT.Sigmoid)
+
+        two_l = load_list("two_l", two)
+        for r in range(4):
+            nc.scalar.dma_start(xs_win[r:P:32, :].bitcast(I32), x_scales[0, r:16:4, :].bitcast(I32))
+        xw_win = sb("xw_win", [P, T], I32)
+        nc.sync.dma_start(xw_win[:], x_words[0].rearrange("p n t -> p (n t)").bitcast(I32))
+        offs_l = load_list("offs_l", offs)
+
+        def load_weight(name, w):
+            halves = []
+            for hh in range(2):
+                raw = sb("%s_raw%d" % (name, hh), [P, 4, 256], F32)
+                nc.sync.dma_start(raw[:], w.rearrange("(p j) c -> p j c", j=4)[:, :, 256 * hh : 256 * (hh + 1)])
+                halves.append(raw)
+            return halves
+
+        w2_raw = load_weight("w2", w2)
+        k1_l = load_list("k1_l", k1)
+        for e in range(2):
+            nc.sync.dma_start(ds_win[e:P:16, :].bitcast(I32), d_scales[0, e:16:2, :].bitcast(I32))
+        w1_raw = load_weight("w1", w1)
+        n2_l = load_list("n2_l", n2)
+        n1_l = load_list("n1_l", n1)
+        dw_win = sb("dw_win", [P, G], I32)
+        nc.sync.dma_start(dw_win[:], d_words[0].rearrange("p n t -> p (n t)").bitcast(I32))
+        n3_l = load_list("n3_l", n3)
+        n4_l = load_list("n4_l", n4)
+
+        gs_t = sb("gs_t", [P, NT], F32)
+        with nc.allow_non_contiguous_dma(reason="one gain a partition and tile"):
+            for c in range(4):
+                nc.gpsimd.dma_start(gs_t[c:P:4, :], gs.rearrange("(a t c) o -> c a (t o)", t=4, c=4)[c])
+
+        ident = sb("ident", [P, P], F32)
+        make_identity(nc, ident[:])
+        d_win = [sb("d_win%d" % t, [P, 2 * S], F32) for t in range(NT)]
+        h_win = [sb("h_win%d" % t, [P, 2 * S], F32) for t in range(NT)]
+        for t in range(NT):
+            nc.vector.memset(d_win[t][:, S:], 0.0)
+        nc.vector.memset(ds_plane[:].bitcast(I32), 0)
+        for t in range(NT):
+            nc.gpsimd.memset(h_win[t][:, S:], 0.0)
+
+        def gather(name, dtype, window, offsets):
+            picked = sb(name, [P, S], dtype)
+            nc.vector.tensor_copy(picked[:], window.indirect(offsets[:]))
+            return picked
+
+        xs_two = gather("xs_two", U8, xs_win[:], two_l)
+        xs_offs = gather("xs_offs", U8, xs_win[:], offs_l)
+        xw_two = gather("xw_two", U32, xw_win[:].bitcast(U32), two_l)
+        xw_offs = gather("xw_offs", U32, xw_win[:].bitcast(U32), offs_l)
+
+        def cast_weight(name, halves):
+            grouped = sb(name + "_bf", [P, 4 * H], BF16)
+            dst = grouped[:].rearrange("p (t a c j) -> p t a c j", t=4, c=4, j=4)
+            for hh in range(2):
+                nc.scalar.copy(dst[:, :, 16 * hh : 16 * (hh + 1)], halves[hh][:].rearrange("p j (a t c) -> p t a c j", t=4, c=4))
+            return grouped
+
+        def quantize(name, grouped):
+            codes = sb(name + "_codes", [P, H], U32)
+            scales = sb(name + "_scales", [P, H], U8)
+            nc.vector.quantize_mx(codes[:].bitcast(FP8X4), scales[:], grouped[:])
+            return codes, scales
+
+        def product(dst, lhs, lhs_scale, rhs, rhs_scale):
+            nc.tensor.matmul_mx(dst, lhsT=lhs.bitcast(FP8X4), lhsT_scale=lhs_scale, rhs=rhs.bitcast(FP8X4), rhs_scale=rhs_scale, start=True, stop=True)
+
+        w2_bf = cast_weight("w2", w2_raw)
+        w2_codes, w2_scales = quantize("w2", w2_bf)
+        d_ps = [bank(t, "d_ps%d" % t) for t in range(NT)]
+        for t in range(NT):
+            cols = slice(P * t, P * (t + 1))
+            product(d_ps[t][:], w2_codes[:, cols], w2_scales[:, cols], xw_two[:], xs_two[:])
+
+        ds_picked = gather("ds_picked", U8, ds_win[:], k1_l)
+        ds_dealt = sb("ds_dealt", [P, H], U8)
+        nc.vector.tensor_copy(ds_dealt[:].rearrange("p (t m) -> p m t", t=4), ds_picked[:].rearrange("p (m t) -> p m t", t=4))
+        for o in range(2):
+            for e in range(2):
+                nc.sync.dma_start(ds_plane[2 * o + e : P : 32, :].bitcast(I32), ds_dealt[16 * o + e : P : 32, :].bitcast(I32))
+
+        nc.scalar.copy(d_win[0][:, :S], d_ps[0][:])
+        w1_bf = cast_weight("w1", w1_raw)
+        for t in range(1, NT):
+            nc.scalar.copy(d_win[t][:, :S], d_ps[t][:])
+        w1_codes, w1_scales = quantize("w1", w1_bf)
+        y_ps = [bank(4 + t, "y_ps%d" % t) for t in range(NT)]
+        for t in range(NT):
+            cols = slice(P * t, P * (t + 1))
+            product(y_ps[t][:], w1_codes[:, cols], w1_scales[:, cols], xw_offs[:], xs_offs[:])
+        y_win = [sb("y_win%d" % t, [P, S], F32) for t in range(NT)]
+        for t in range(NT):
+            nc.scalar.activation(y_win[t][:], y_ps[t][:], ACT.Copy, scale=gs_t[:, t : t + 1])
+
+        ds_ps = [bank(b, "ds_ps%d" % b) for b in range(4)]
+        d_nb = []
+        for t in range(NT):
+            d_nb.append(gather("d_nb%d" % t, F32, d_win[t][:], n2_l))
+        for t in range(NT):
+            for b in range(4):
+                add_transpose(ds_ps[b][:, P * t : P * (t + 1)], d_win[t][:, P * b : P * (b + 1)], t == 0, False)
+            for b in range(4):
+                add_transpose(ds_ps[b][:, P * t : P * (t + 1)], d_nb[t][:, P * b : P * (b + 1)], False, t == NT - 1)
+        gate = [sb("gate%d" % b, [P, K], F32) for b in range(4)]
+        for b in range(4):
+            nc.scalar.activation(gate[b][:].rearrange("p (a t c) -> p a t c", t=4, c=4), ds_ps[b][:].rearrange("p (t a c) -> p a t c", t=4, c=4), ACT.Sigmoid)
+        warm2 = sb("warm2", [P, 1], F32)
+        nc.scalar.activation(warm2[:], gate[3][:, 0:1], ACT.Abs_reciprocal_sqrt, bias=1.0)
+
+        ys_ps = [bank(4 + b, "ys_ps%d" % b) for b in range(4)]
+        y_nb = [sb("y_nb%d" % t, [P, FIRST], F32) for t in range(NT)]
+        y_nb_last = [sb("y_nb_last%d" % t, [P, S - FIRST], F32) for t in range(NT)]
+        for t in range(NT):
+            nc.vector.tensor_copy(y_nb[t][:], y_win[t][:].indirect(n1_l[:, : FIRST // 16]))
+        for t in range(NT):
+            nc.vector.tensor_copy(y_nb_last[t][:], y_win[t][:].indirect(n1_l[:, FIRST // 16 :]))
+        for t in range(NT):
+            for b in range(4):
+                add_transpose(ys_ps[b][:, P * t : P * (t + 1)], y_win[t][:, P * b : P * (b + 1)], t == 0, False)
+            for b in range(3):
+                add_transpose(ys_ps[b][:, P * t : P * (t + 1)], y_nb[t][:, P * b : P * (b + 1)], False, t == NT - 1)
+        for t in range(NT):
+            add_transpose(ys_ps[3][:, P * t : P * (t + 1)], y_nb_last[t][:], False, t == NT - 1)
+
+        z_rows = [sb("z_rows%d" % b, [P, K], BF16) for b in range(4)]
+        z_bf = [sb("z_bf%d" % b, [P, 4 * P], BF16) for b in range(4)]
+        z_codes = [sb("z_codes%d" % b, [P, P], U32) for b in range(4)]
+        z_scales = [sb("z_scales%d" % b, [P, P], U8) for b in range(4)]
+        h_ps = [bank(t, "h_ps%d" % t) for t in range(NT)]
+
+        for b in range(4):
+            nc.vector.tensor_tensor(
+                z_rows[b][:].rearrange("p (a t c) -> p a t c", t=4, c=4),
+                ys_ps[b][:].rearrange("p (t a c) -> p a t c", t=4, c=4),
+                gate[b][:].rearrange("p (a t c) -> p a t c", t=4, c=4),
+                ALU.mult,
+            )
+            pairs = bank(4 + b, "pairs%d" % b)
+            words = z_rows[b][:].bitcast(F32)
+            for u in range(2):
+                nc.tensor.transpose(pairs[:, P * u : P * (u + 1)], words[:, u : 2 * P : 2], ident[:])
+            nc.scalar.copy(
+                z_bf[b][:].bitcast(F32).rearrange("p (j u) -> p j u", u=2),
+                pairs[:, : 2 * P].rearrange("p (u j) -> p j u", u=2),
+            )
+
+        dw_picked = gather("dw_picked", U32, dw_win[:].bitcast(U32), k1_l)
+        dw_dealt = sb("dw_dealt", [P, H], U32)
+        nc.vector.tensor_copy(dw_dealt[:].rearrange("p (t m) -> p m t", t=4), dw_picked[:].rearrange("p (m t) -> p m t", t=4))
+
+        for b in range(4):
+            nc.vector.quantize_mx(z_codes[b][:].bitcast(FP8X4), z_scales[b][:], z_bf[b][:])
+            for t in range(NT):
+                cols = slice(P * t, P * (t + 1))
+                product(h_ps[t][:, P * b : P * (b + 1)], dw_dealt[:, cols], ds_plane[:, cols], z_codes[b][:], z_scales[b][:])
+            if b == 2:
+                for t in range(NT):
+                    nc.scalar.copy(h_win[t][:, :FIRST], h_ps[t][:, :FIRST])
+        for t in range(NT):
+            nc.scalar.copy(h_win[t][:, FIRST:S], h_ps[t][:, FIRST:])
+
+        out_rows = out.rearrange("(p t) j -> t p j", t=4)
+        stage = {}
+
+        def front(t):
+            pa = sb("pa%d" % t, [P, S], F32)
+            pb = sb("pb%d" % t, [P, S], F32)
+            nc.vector.tensor_scalar(pa[:], h_win[t][:].indirect(n3_l[:]), ALPHA, 0.0, ALU.mult, ALU.add)
+            nc.vector.tensor_scalar(pb[:], h_win[t][:].indirect(n4_l[:]), -ALPHA, 0.0, ALU.mult, ALU.add)
+            diff_ps = bank((3 * t + 4) % 8, "diff_ps%d" % t)
+            for b in range(4):
+                cols = slice(P * b, P * (b + 1))
+                add_transpose(diff_ps[:, cols], pa[:, cols], True, False)
+                add_transpose(diff_ps[:, cols], pb[:, cols], False, True)
+            diff_sq = sb("diff_sq%d" % t, [P, S], F32)
+            nc.scalar.activation(diff_sq[:], diff_ps[:], ACT.Square, scale=HS / (ALPHA * math.sqrt(2.0)))
+            stage[t] = (pa, pb, diff_sq)
+
+        def middle(t):
+            pa, pb, diff_sq = stage[t]
+            both = sb("both%d" % t, [P, S], F32)
+            nc.vector.tensor_tensor(both[:], pb[:], pa[:], ALU.subtract)
+            top = sb("top%d" % t, [P, S], F32)
+            nc.vector.scalar_tensor_tensor(top[:], both[:], 1.0 / (2.2 * ALPHA), h_win[t][:, :S], ALU.mult, ALU.add)
+            mean_ps = bank((3 * t + 5) % 8, "mean_ps%d" % t)
+            for b in range(4):
+                cols = slice(P * b, P * (b + 1))
+                add_transpose(mean_ps[:, cols], both[:, cols], True, False)
+                add_transpose(mean_ps[:, cols], top[:, cols], False, True)
+            mean_sq = sb("mean_sq%d" % t, [P, S], F32)
+            nc.scalar.activation(mean_sq[:], mean_ps[:], ACT.Square, scale=HS * 0.3125 * math.sqrt(2.0))
+            var_ps = bank((3 * t + 6) % 8, "var_ps%d" % t)
+            for b in range(4):
+                cols = slice(P * b, P * (b + 1))
+                add_transpose(var_ps[:, cols], diff_sq[:, cols], True, False)
+                add_transpose(var_ps[:, cols], mean_sq[:, cols], False, True)
+            inv = sb("inv%d" % t, [P, S], F32)
+            nc.scalar.activation(inv[:], var_ps[:], ACT.Abs_reciprocal_sqrt, bias=0.25)
+            stage[t] = (top, inv)
+
+        def back(t):
+            top, inv = stage[t]
+            res = sb("res%d" % t, [P, S], F32)
+            nc.vector.scalar_tensor_tensor(res[:], top[:], HS * 0.6875, inv[:], ALU.mult, ALU.mult)
+            nc.sync.dma_start(out_rows[t], res[:])
+
+        for t in range(NT + 2):
+            if t < NT:
+                front(t)
+            if 1 <= t <= NT:
+                middle(t - 1)
+            if t >= 2:
+                back(t - 2)

@@ -50,7 +50,7 @@ def tile_picked_twqtriebstd_none_p_kernel(
         xs_win = sb("xs_win", [P, T], U8)
         ds_win = sb("ds_win", [P, G], U8)
         ds_plane = sb("ds_plane", [P, H], U8)
-        nc.vector.memset(xs_win[:].bitcast(I32), 0)
+        nc.gpsimd.memset(xs_win[:].bitcast(I32), 0)
         nc.vector.memset(ds_win[:].bitcast(I32), 0)
         warm = sb("warm", [P, 2], F32)
         nc.vector.memset(warm[:, 0:1], 0.0)
@@ -58,10 +58,10 @@ def tile_picked_twqtriebstd_none_p_kernel(
 
         two_l = load_list("two_l", two)
         for r in range(4):
-            nc.scalar.dma_start(xs_win[r:P:32, :].bitcast(I32), x_scales[0, r:16:4, :].bitcast(I32))
+            queue = nc.scalar if r % 2 else nc.sync
+            queue.dma_start(xs_win[r:P:32, :].bitcast(I32), x_scales[0, r:16:4, :].bitcast(I32))
         xw_win = sb("xw_win", [P, T], I32)
         nc.sync.dma_start(xw_win[:], x_words[0].rearrange("p n t -> p (n t)").bitcast(I32))
-        offs_l = load_list("offs_l", offs)
 
         def load_weight(name, w):
             halves = []
@@ -72,21 +72,21 @@ def tile_picked_twqtriebstd_none_p_kernel(
             return halves
 
         w2_raw = load_weight("w2", w2)
+        offs_l = load_list("offs_l", offs)
         k1_l = load_list("k1_l", k1)
         for e in range(2):
             nc.sync.dma_start(ds_win[e:P:16, :].bitcast(I32), d_scales[0, e:16:2, :].bitcast(I32))
         w1_raw = load_weight("w1", w1)
         n2_l = load_list("n2_l", n2)
+        gs_t = sb("gs_t", [P, NT], F32)
+        with nc.allow_non_contiguous_dma(reason="one gain a partition and tile"):
+            for c in range(4):
+                nc.sync.dma_start(gs_t[c:P:4, :], gs.rearrange("(a t c) o -> c a (t o)", t=4, c=4)[c])
         n1_l = load_list("n1_l", n1)
         dw_win = sb("dw_win", [P, G], I32)
         nc.sync.dma_start(dw_win[:], d_words[0].rearrange("p n t -> p (n t)").bitcast(I32))
         n3_l = load_list("n3_l", n3)
         n4_l = load_list("n4_l", n4)
-
-        gs_t = sb("gs_t", [P, NT], F32)
-        with nc.allow_non_contiguous_dma(reason="one gain a partition and tile"):
-            for c in range(4):
-                nc.gpsimd.dma_start(gs_t[c:P:4, :], gs.rearrange("(a t c) o -> c a (t o)", t=4, c=4)[c])
 
         ident = sb("ident", [P, P], F32)
         make_identity(nc, ident[:])
@@ -95,8 +95,6 @@ def tile_picked_twqtriebstd_none_p_kernel(
         for t in range(NT):
             nc.vector.memset(d_win[t][:, S:], 0.0)
         nc.vector.memset(ds_plane[:].bitcast(I32), 0)
-        for t in range(NT):
-            nc.gpsimd.memset(h_win[t][:, S:], 0.0)
 
         def gather(name, dtype, window, offsets):
             picked = sb(name, [P, S], dtype)
@@ -104,9 +102,7 @@ def tile_picked_twqtriebstd_none_p_kernel(
             return picked
 
         xs_two = gather("xs_two", U8, xs_win[:], two_l)
-        xs_offs = gather("xs_offs", U8, xs_win[:], offs_l)
         xw_two = gather("xw_two", U32, xw_win[:].bitcast(U32), two_l)
-        xw_offs = gather("xw_offs", U32, xw_win[:].bitcast(U32), offs_l)
 
         def cast_weight(name, halves):
             grouped = sb(name + "_bf", [P, 4 * H], BF16)
@@ -131,9 +127,11 @@ def tile_picked_twqtriebstd_none_p_kernel(
             cols = slice(P * t, P * (t + 1))
             product(d_ps[t][:], w2_codes[:, cols], w2_scales[:, cols], xw_two[:], xs_two[:])
 
+        xs_offs = gather("xs_offs", U8, xs_win[:], offs_l)
+        xw_offs = gather("xw_offs", U32, xw_win[:].bitcast(U32), offs_l)
         ds_picked = gather("ds_picked", U8, ds_win[:], k1_l)
         ds_dealt = sb("ds_dealt", [P, H], U8)
-        nc.vector.tensor_copy(ds_dealt[:].rearrange("p (t m) -> p m t", t=4), ds_picked[:].rearrange("p (m t) -> p m t", t=4))
+        nc.vector.tensor_copy(ds_dealt[:].rearrange("p (t q i) -> p q t i", t=4, i=16), ds_picked[:].rearrange("p (q i t) -> p q t i", t=4, i=16))
         for o in range(2):
             for e in range(2):
                 nc.sync.dma_start(ds_plane[2 * o + e : P : 32, :].bitcast(I32), ds_dealt[16 * o + e : P : 32, :].bitcast(I32))
@@ -152,9 +150,9 @@ def tile_picked_twqtriebstd_none_p_kernel(
             nc.scalar.activation(y_win[t][:], y_ps[t][:], ACT.Copy, scale=gs_t[:, t : t + 1])
 
         ds_ps = [bank(b, "ds_ps%d" % b) for b in range(4)]
-        d_nb = []
+        d_nb = [h_win[t][:, S:] for t in range(NT)]
         for t in range(NT):
-            d_nb.append(gather("d_nb%d" % t, F32, d_win[t][:], n2_l))
+            nc.vector.tensor_copy(d_nb[t], d_win[t][:].indirect(n2_l[:]))
         for t in range(NT):
             for b in range(4):
                 add_transpose(ds_ps[b][:, P * t : P * (t + 1)], d_win[t][:, P * b : P * (b + 1)], t == 0, False)
@@ -205,7 +203,7 @@ def tile_picked_twqtriebstd_none_p_kernel(
 
         dw_picked = gather("dw_picked", U32, dw_win[:].bitcast(U32), k1_l)
         dw_dealt = sb("dw_dealt", [P, H], U32)
-        nc.vector.tensor_copy(dw_dealt[:].rearrange("p (t m) -> p m t", t=4), dw_picked[:].rearrange("p (m t) -> p m t", t=4))
+        nc.vector.tensor_copy(dw_dealt[:].rearrange("p (t q i) -> p q t i", t=4, i=4), dw_picked[:].rearrange("p (q i t) -> p q t i", t=4, i=4))
 
         for b in range(4):
             nc.vector.quantize_mx(z_codes[b][:].bitcast(FP8X4), z_scales[b][:], z_bf[b][:])
@@ -219,54 +217,61 @@ def tile_picked_twqtriebstd_none_p_kernel(
             nc.scalar.copy(h_win[t][:, FIRST:S], h_ps[t][:, FIRST:])
 
         out_rows = out.rearrange("(p t) j -> t p j", t=4)
-        stage = {}
+        pieces = [(0, 0, S), (1, 0, S), (2, 0, S), (3, 0, S // 2), (3, S // 2, S)]
+        tiles = {}
 
-        def front(t):
-            pa = sb("pa%d" % t, [P, S], F32)
-            pb = sb("pb%d" % t, [P, S], F32)
-            nc.vector.tensor_scalar(pa[:], h_win[t][:].indirect(n3_l[:]), ALPHA, 0.0, ALU.mult, ALU.add)
-            nc.vector.tensor_scalar(pb[:], h_win[t][:].indirect(n4_l[:]), -ALPHA, 0.0, ALU.mult, ALU.add)
-            diff_ps = bank((3 * t + 4) % 8, "diff_ps%d" % t)
-            for b in range(4):
-                cols = slice(P * b, P * (b + 1))
-                add_transpose(diff_ps[:, cols], pa[:, cols], True, False)
-                add_transpose(diff_ps[:, cols], pb[:, cols], False, True)
-            diff_sq = sb("diff_sq%d" % t, [P, S], F32)
-            nc.scalar.activation(diff_sq[:], diff_ps[:], ACT.Square, scale=HS / (ALPHA * math.sqrt(2.0)))
-            stage[t] = (pa, pb, diff_sq)
+        def piece_tile(name, n):
+            t, lo, hi = pieces[n]
+            tiles[name, n] = sb("%s%d" % (name, n), [P, hi - lo], F32)
+            return tiles[name, n]
 
-        def middle(t):
-            pa, pb, diff_sq = stage[t]
-            both = sb("both%d" % t, [P, S], F32)
-            nc.vector.tensor_tensor(both[:], pb[:], pa[:], ALU.subtract)
-            top = sb("top%d" % t, [P, S], F32)
-            nc.vector.scalar_tensor_tensor(top[:], both[:], 1.0 / (2.2 * ALPHA), h_win[t][:, :S], ALU.mult, ALU.add)
-            mean_ps = bank((3 * t + 5) % 8, "mean_ps%d" % t)
-            for b in range(4):
-                cols = slice(P * b, P * (b + 1))
-                add_transpose(mean_ps[:, cols], both[:, cols], True, False)
-                add_transpose(mean_ps[:, cols], top[:, cols], False, True)
-            mean_sq = sb("mean_sq%d" % t, [P, S], F32)
-            nc.scalar.activation(mean_sq[:], mean_ps[:], ACT.Square, scale=HS * 0.3125 * math.sqrt(2.0))
-            var_ps = bank((3 * t + 6) % 8, "var_ps%d" % t)
-            for b in range(4):
-                cols = slice(P * b, P * (b + 1))
-                add_transpose(var_ps[:, cols], diff_sq[:, cols], True, False)
-                add_transpose(var_ps[:, cols], mean_sq[:, cols], False, True)
-            inv = sb("inv%d" % t, [P, S], F32)
-            nc.scalar.activation(inv[:], var_ps[:], ACT.Abs_reciprocal_sqrt, bias=0.25)
-            stage[t] = (top, inv)
+        def add_both(n, name, slot, first, second):
+            t, lo, hi = pieces[n]
+            acc = bank((3 * n + 4 + slot) % 8, "%s%d" % (name, n))
+            for c in range(0, hi - lo, P):
+                add_transpose(acc[:, c : c + P], first[:, c : c + P], True, False)
+                add_transpose(acc[:, c : c + P], second[:, c : c + P], False, True)
+            return acc[:, : hi - lo]
 
-        def back(t):
-            top, inv = stage[t]
-            res = sb("res%d" % t, [P, S], F32)
-            nc.vector.scalar_tensor_tensor(res[:], top[:], HS * 0.6875, inv[:], ALU.mult, ALU.mult)
-            nc.sync.dma_start(out_rows[t], res[:])
+        def fetch_a(n):
+            t, lo, hi = pieces[n]
+            nc.vector.tensor_scalar(piece_tile("pa", n)[:], h_win[t][:].indirect(n3_l[:, lo // 16 : hi // 16]), ALPHA, 0.0, ALU.mult, ALU.add)
 
-        for t in range(NT + 2):
-            if t < NT:
-                front(t)
-            if 1 <= t <= NT:
-                middle(t - 1)
-            if t >= 2:
-                back(t - 2)
+        def fetch_b(n):
+            t, lo, hi = pieces[n]
+            nc.vector.tensor_scalar(piece_tile("pb", n)[:], h_win[t][:].indirect(n4_l[:, lo // 16 : hi // 16]), -ALPHA, 0.0, ALU.mult, ALU.add)
+            diff = add_both(n, "diff_ps", 0, tiles["pa", n], tiles["pb", n])
+            nc.scalar.activation(piece_tile("diff_sq", n)[:], diff, ACT.Square, scale=HS / (ALPHA * math.sqrt(2.0)))
+
+        def sum_pair(n):
+            nc.vector.tensor_tensor(piece_tile("both", n)[:], tiles["pb", n][:], tiles["pa", n][:], ALU.subtract)
+
+        def centre(n):
+            t, lo, hi = pieces[n]
+            top = piece_tile("top", n)
+            nc.vector.scalar_tensor_tensor(top[:], tiles["both", n][:], 1.0 / (2.2 * ALPHA), h_win[t][:, lo:hi], ALU.mult, ALU.add)
+            mean = add_both(n, "mean_ps", 1, tiles["both", n], top)
+            nc.scalar.activation(piece_tile("mean_sq", n)[:], mean, ACT.Square, scale=HS * 0.3125 * math.sqrt(2.0))
+            var = add_both(n, "var_ps", 2, tiles["diff_sq", n], tiles["mean_sq", n])
+            nc.scalar.activation(piece_tile("inv", n)[:], var, ACT.Abs_reciprocal_sqrt, bias=0.25)
+
+        def finish(n):
+            t, lo, hi = pieces[n]
+            res = piece_tile("res", n)
+            nc.vector.scalar_tensor_tensor(res[:], tiles["top", n][:], HS * 0.6875, tiles["inv", n][:], ALU.mult, ALU.mult)
+            nc.sync.dma_start(out_rows[t][:, lo:hi], res[:])
+
+        last = len(pieces) - 1
+        fetch_a(0)
+        fetch_b(0)
+        for n in range(last):
+            fetch_a(n + 1)
+            sum_pair(n)
+            fetch_b(n + 1)
+            centre(n)
+        finish(0)
+        sum_pair(last)
+        finish(1)
+        centre(last)
+        for n in range(2, last + 1):
+            finish(n)

@@ -22,6 +22,7 @@ NT = 4
 FIRST = 384
 ALPHA = 8.0 / 55.0
 HS = 0.0625
+BANKS = [(4, 5, 6), (7, 4, 5), (0, 6, 7), (1, 4, 5), (2, 6, 7)]
 
 
 def tile_picked_twqtriebstd_none_p_kernel(
@@ -93,7 +94,7 @@ def tile_picked_twqtriebstd_none_p_kernel(
         d_win = [sb("d_win%d" % t, [P, 2 * S], F32) for t in range(NT)]
         h_win = [sb("h_win%d" % t, [P, 2 * S], F32) for t in range(NT)]
         for t in range(NT):
-            nc.vector.memset(d_win[t][:, S:], 0.0)
+            nc.gpsimd.memset(d_win[t][:, S:], 0.0)
         nc.vector.memset(ds_plane[:].bitcast(I32), 0)
 
         def gather(name, dtype, window, offsets):
@@ -146,8 +147,10 @@ def tile_picked_twqtriebstd_none_p_kernel(
             cols = slice(P * t, P * (t + 1))
             product(y_ps[t][:], w1_codes[:, cols], w1_scales[:, cols], xw_offs[:], xs_offs[:])
         y_win = [sb("y_win%d" % t, [P, S], F32) for t in range(NT)]
+        y_own = [sb("y_own%d" % t, [P, S], F32) for t in range(NT)]
         for t in range(NT):
             nc.scalar.activation(y_win[t][:], y_ps[t][:], ACT.Copy, scale=gs_t[:, t : t + 1])
+            nc.scalar.activation(y_own[t][:], y_ps[t][:], ACT.Copy, scale=gs_t[:, t : t + 1])
 
         ds_ps = [bank(b, "ds_ps%d" % b) for b in range(4)]
         d_nb = [h_win[t][:, S:] for t in range(NT)]
@@ -165,19 +168,13 @@ def tile_picked_twqtriebstd_none_p_kernel(
         nc.scalar.activation(warm2[:], gate[3][:, 0:1], ACT.Abs_reciprocal_sqrt, bias=1.0)
 
         ys_ps = [bank(4 + b, "ys_ps%d" % b) for b in range(4)]
-        y_nb = [sb("y_nb%d" % t, [P, FIRST], F32) for t in range(NT)]
-        y_nb_last = [sb("y_nb_last%d" % t, [P, S - FIRST], F32) for t in range(NT)]
-        for t in range(NT):
-            nc.vector.tensor_copy(y_nb[t][:], y_win[t][:].indirect(n1_l[:, : FIRST // 16]))
-        for t in range(NT):
-            nc.vector.tensor_copy(y_nb_last[t][:], y_win[t][:].indirect(n1_l[:, FIRST // 16 :]))
-        for t in range(NT):
-            for b in range(4):
-                add_transpose(ys_ps[b][:, P * t : P * (t + 1)], y_win[t][:, P * b : P * (b + 1)], t == 0, False)
-            for b in range(3):
-                add_transpose(ys_ps[b][:, P * t : P * (t + 1)], y_nb[t][:, P * b : P * (b + 1)], False, t == NT - 1)
-        for t in range(NT):
-            add_transpose(ys_ps[3][:, P * t : P * (t + 1)], y_nb_last[t][:], False, t == NT - 1)
+        for half in range(2):
+            lo, hi = 2 * P * half, 2 * P * (half + 1)
+            for t in range(NT):
+                y_sum = sb("y_sum%d_%d" % (half, t), [P, 2 * P], F32)
+                nc.vector.tensor_tensor(y_sum[:], y_win[t][:].indirect(n1_l[:, lo // 16 : hi // 16]), y_own[t][:, lo:hi], ALU.add)
+                for i in range(2):
+                    nc.tensor.transpose(ys_ps[2 * half + i][:, P * t : P * (t + 1)], y_sum[:, P * i : P * (i + 1)], ident[:])
 
         z_rows = [sb("z_rows%d" % b, [P, K], BF16) for b in range(4)]
         z_bf = [sb("z_bf%d" % b, [P, 4 * P], BF16) for b in range(4)]
@@ -212,9 +209,9 @@ def tile_picked_twqtriebstd_none_p_kernel(
                 product(h_ps[t][:, P * b : P * (b + 1)], dw_dealt[:, cols], ds_plane[:, cols], z_codes[b][:], z_scales[b][:])
             if b == 2:
                 for t in range(NT):
-                    nc.scalar.copy(h_win[t][:, :FIRST], h_ps[t][:, :FIRST])
+                    nc.scalar.activation(h_win[t][:, :FIRST], h_ps[t][:, :FIRST], ACT.Copy, scale=ALPHA)
         for t in range(NT):
-            nc.scalar.copy(h_win[t][:, FIRST:S], h_ps[t][:, FIRST:])
+            nc.scalar.activation(h_win[t][:, FIRST:S], h_ps[t][:, FIRST:], ACT.Copy, scale=ALPHA)
 
         out_rows = out.rearrange("(p t) j -> t p j", t=4)
         pieces = [(0, 0, S), (1, 0, S), (2, 0, S), (3, 0, S // 2), (3, S // 2, S)]
@@ -227,29 +224,30 @@ def tile_picked_twqtriebstd_none_p_kernel(
 
         def add_both(n, name, slot, first, second):
             t, lo, hi = pieces[n]
-            acc = bank((3 * n + 4 + slot) % 8, "%s%d" % (name, n))
+            acc = bank(BANKS[n][slot], "%s%d" % (name, n))
             for c in range(0, hi - lo, P):
-                add_transpose(acc[:, c : c + P], first[:, c : c + P], True, False)
-                add_transpose(acc[:, c : c + P], second[:, c : c + P], False, True)
+                add_transpose(acc[:, c : c + P], first[:, c : c + P], True, second is None)
+                if second is not None:
+                    add_transpose(acc[:, c : c + P], second[:, c : c + P], False, True)
             return acc[:, : hi - lo]
 
         def fetch_a(n):
             t, lo, hi = pieces[n]
-            nc.vector.tensor_scalar(piece_tile("pa", n)[:], h_win[t][:].indirect(n3_l[:, lo // 16 : hi // 16]), ALPHA, 0.0, ALU.mult, ALU.add)
+            nc.vector.tensor_copy(piece_tile("pa", n)[:], h_win[t][:].indirect(n3_l[:, lo // 16 : hi // 16]))
 
         def fetch_b(n):
             t, lo, hi = pieces[n]
-            nc.vector.tensor_scalar(piece_tile("pb", n)[:], h_win[t][:].indirect(n4_l[:, lo // 16 : hi // 16]), -ALPHA, 0.0, ALU.mult, ALU.add)
-            diff = add_both(n, "diff_ps", 0, tiles["pa", n], tiles["pb", n])
+            nc.vector.tensor_tensor(piece_tile("diff", n)[:], h_win[t][:].indirect(n4_l[:, lo // 16 : hi // 16]), tiles["pa", n][:], ALU.subtract)
+            diff = add_both(n, "diff_ps", 0, tiles["diff", n], None)
             nc.scalar.activation(piece_tile("diff_sq", n)[:], diff, ACT.Square, scale=HS / (ALPHA * math.sqrt(2.0)))
 
         def sum_pair(n):
-            nc.vector.tensor_tensor(piece_tile("both", n)[:], tiles["pb", n][:], tiles["pa", n][:], ALU.subtract)
+            nc.vector.scalar_tensor_tensor(piece_tile("both", n)[:], tiles["pa", n][:], 2.0, tiles["diff", n][:], ALU.mult, ALU.add)
 
         def centre(n):
             t, lo, hi = pieces[n]
             top = piece_tile("top", n)
-            nc.vector.scalar_tensor_tensor(top[:], tiles["both", n][:], 1.0 / (2.2 * ALPHA), h_win[t][:, lo:hi], ALU.mult, ALU.add)
+            nc.vector.scalar_tensor_tensor(top[:], tiles["both", n][:], 1.0 / (2.2 * ALPHA), h_ps[t][:, lo:hi], ALU.mult, ALU.subtract)
             mean = add_both(n, "mean_ps", 1, tiles["both", n], top)
             nc.scalar.activation(piece_tile("mean_sq", n)[:], mean, ACT.Square, scale=HS * 0.3125 * math.sqrt(2.0))
             var = add_both(n, "var_ps", 2, tiles["diff_sq", n], tiles["mean_sq", n])
@@ -258,7 +256,7 @@ def tile_picked_twqtriebstd_none_p_kernel(
         def finish(n):
             t, lo, hi = pieces[n]
             res = piece_tile("res", n)
-            nc.vector.scalar_tensor_tensor(res[:], tiles["top", n][:], HS * 0.6875, tiles["inv", n][:], ALU.mult, ALU.mult)
+            nc.vector.scalar_tensor_tensor(res[:], tiles["top", n][:], -HS * 0.6875, tiles["inv", n][:], ALU.mult, ALU.mult)
             nc.sync.dma_start(out_rows[t][:, lo:hi], res[:])
 
         last = len(pieces) - 1

@@ -18,11 +18,21 @@ ALU = mybir.AluOpType
 ACT = mybir.ActivationFunctionType
 
 P = 128
-NT = 4
-FIRST = 384
-ALPHA = 8.0 / 55.0
-HS = 0.0625
-BANKS = [(4, 5, 6), (7, 4, 5), (0, 6, 7), (1, 4, 5), (2, 6, 7)]
+TILES = 4
+BLOCKS = S // P
+WINDOW = 2 * S
+HALF = H // 2
+
+H_FACTOR = 0.0625
+WINDOW_FACTOR = 0.6 - 1.0 / 2.2
+TOP_FACTOR = 1.0 / (2.2 * WINDOW_FACTOR)
+MEAN_FACTOR = 0.6 / WINDOW_FACTOR
+DIFF_SCALE = H_FACTOR / (WINDOW_FACTOR * math.sqrt(2.0))
+MEAN_SCALE = H_FACTOR * 0.3125 * math.sqrt(2.0)
+OUT_FACTOR = -H_FACTOR * 0.6875
+
+LAST = TILES - 1
+NORM_BANKS = [(0, 1, 2), (3, 0, 1), (4, 3, 2)]
 
 
 def tile_picked_twqtriebstd_none_p_kernel(
@@ -34,19 +44,35 @@ def tile_picked_twqtriebstd_none_p_kernel(
         keep = ctx.enter_context(tc.tile_pool(name="keep", bufs=1))
         psum = ctx.enter_context(tc.psum_pool(name="psum", bufs=1))
 
-        def sb(name, shape, dtype):
-            return keep.tile(shape, dtype, name=name, align_bytes=64)
+        def sb(name, shape, dtype, slot=None):
+            return keep.tile(shape, dtype, name=name, tag=slot or name, align_bytes=64)
 
-        def bank(b, name):
-            return psum.tile([P, 512], F32, name=name, tag="bank%d" % b)
+        def bank(index, name):
+            return psum.tile([P, 512], F32, name=name, tag="bank%d" % index)
+
+        def block(i):
+            return slice(P * i, P * (i + 1))
 
         def load_list(name, src):
             tile = lists.tile([P, S // 16], U16, name=name)
             nc.sync.dma_start(tile[:], src)
             return tile
 
+        def load_half(name, w, half):
+            raw = sb("%s_raw%d" % (name, half), [P, 4, HALF], F32)
+            nc.sync.dma_start(raw[:], w.rearrange("(p j) c -> p j c", j=4)[:, :, HALF * half : HALF * (half + 1)])
+            return raw
+
         def add_transpose(dst, src, start, stop):
             nc.tensor.matmul(dst, src, ident[:], start=start, stop=stop, is_transpose=True)
+
+        def gather(name, dtype, window, offsets, slot=None):
+            picked = sb(name, [P, S], dtype, slot)
+            nc.vector.tensor_copy(picked[:], window.indirect(offsets[:]))
+            return picked
+
+        def product(dst, lhs, lhs_scale, rhs, rhs_scale):
+            nc.tensor.matmul_mx(dst, lhsT=lhs.bitcast(FP8X4), lhsT_scale=lhs_scale, rhs=rhs.bitcast(FP8X4), rhs_scale=rhs_scale, start=True, stop=True)
 
         xs_win = sb("xs_win", [P, T], U8)
         ds_win = sb("ds_win", [P, G], U8)
@@ -58,29 +84,19 @@ def tile_picked_twqtriebstd_none_p_kernel(
         nc.scalar.activation(warm[:, 1:2], warm[:, 0:1], ACT.Sigmoid)
 
         two_l = load_list("two_l", two)
-        for r in range(4):
-            queue = nc.scalar if r % 2 else nc.sync
-            queue.dma_start(xs_win[r:P:32, :].bitcast(I32), x_scales[0, r:16:4, :].bitcast(I32))
-        xw_win = sb("xw_win", [P, T], I32)
-        nc.sync.dma_start(xw_win[:], x_words[0].rearrange("p n t -> p (n t)").bitcast(I32))
-
-        def load_weight(name, w):
-            halves = []
-            for hh in range(2):
-                raw = sb("%s_raw%d" % (name, hh), [P, 4, 256], F32)
-                nc.sync.dma_start(raw[:], w.rearrange("(p j) c -> p j c", j=4)[:, :, 256 * hh : 256 * (hh + 1)])
-                halves.append(raw)
-            return halves
-
-        w2_raw = load_weight("w2", w2)
         offs_l = load_list("offs_l", offs)
         k1_l = load_list("k1_l", k1)
+        xw_win = sb("xw_win", [P, T], I32)
+        nc.sync.dma_start(xw_win[:], x_words[0].rearrange("p n t -> p (n t)").bitcast(I32))
+        for r in range(4):
+            nc.sync.dma_start(xs_win[r:P:32, :].bitcast(I32), x_scales[0, r:16:4, :].bitcast(I32))
+        w2_raw = [load_half("w2", w2, 0), load_half("w2", w2, 1)]
         for e in range(2):
             nc.sync.dma_start(ds_win[e:P:16, :].bitcast(I32), d_scales[0, e:16:2, :].bitcast(I32))
-        w1_raw = load_weight("w1", w1)
         n2_l = load_list("n2_l", n2)
-        gs_t = sb("gs_t", [P, NT], F32)
-        with nc.allow_non_contiguous_dma(reason="one gain a partition and tile"):
+        w1_raw = [load_half("w1", w1, 0), load_half("w1", w1, 1)]
+        gs_t = sb("gs_t", [P, TILES], F32)
+        with nc.allow_non_contiguous_dma(reason="one gain for each partition and tile"):
             for c in range(4):
                 nc.sync.dma_start(gs_t[c:P:4, :], gs.rearrange("(a t c) o -> c a (t o)", t=4, c=4)[c])
         n1_l = load_list("n1_l", n1)
@@ -91,185 +107,190 @@ def tile_picked_twqtriebstd_none_p_kernel(
 
         ident = sb("ident", [P, P], F32)
         make_identity(nc, ident[:])
-        d_win = [sb("d_win%d" % t, [P, 2 * S], F32) for t in range(NT)]
-        h_win = [sb("h_win%d" % t, [P, 2 * S], F32) for t in range(NT)]
-        for t in range(NT):
-            nc.gpsimd.memset(d_win[t][:, S:], 0.0)
+        h_win = [sb("h_win%d" % t, [P, WINDOW], F32) for t in range(TILES)]
         nc.vector.memset(ds_plane[:].bitcast(I32), 0)
-
-        def gather(name, dtype, window, offsets):
-            picked = sb(name, [P, S], dtype)
-            nc.vector.tensor_copy(picked[:], window.indirect(offsets[:]))
-            return picked
 
         xs_two = gather("xs_two", U8, xs_win[:], two_l)
         xw_two = gather("xw_two", U32, xw_win[:].bitcast(U32), two_l)
+        xw_offs = gather("xw_offs", U32, xw_win[:].bitcast(U32), offs_l)
+        xs_offs = gather("xs_offs", U8, xs_win[:], offs_l)
 
         def cast_weight(name, halves):
             grouped = sb(name + "_bf", [P, 4 * H], BF16)
             dst = grouped[:].rearrange("p (t a c j) -> p t a c j", t=4, c=4, j=4)
-            for hh in range(2):
-                nc.scalar.copy(dst[:, :, 16 * hh : 16 * (hh + 1)], halves[hh][:].rearrange("p j (a t c) -> p t a c j", t=4, c=4))
+            for half in range(2):
+                nc.scalar.copy(dst[:, :, 16 * half : 16 * (half + 1)], halves[half][:].rearrange("p j (a t c) -> p t a c j", t=4, c=4))
             return grouped
 
-        def quantize(name, grouped):
+        def quantize_weight(name, grouped):
             codes = sb(name + "_codes", [P, H], U32)
             scales = sb(name + "_scales", [P, H], U8)
             nc.vector.quantize_mx(codes[:].bitcast(FP8X4), scales[:], grouped[:])
             return codes, scales
 
-        def product(dst, lhs, lhs_scale, rhs, rhs_scale):
-            nc.tensor.matmul_mx(dst, lhsT=lhs.bitcast(FP8X4), lhsT_scale=lhs_scale, rhs=rhs.bitcast(FP8X4), rhs_scale=rhs_scale, start=True, stop=True)
+        w2_codes, w2_scales = quantize_weight("w2", cast_weight("w2", w2_raw))
 
-        w2_bf = cast_weight("w2", w2_raw)
-        w2_codes, w2_scales = quantize("w2", w2_bf)
-        d_ps = [bank(t, "d_ps%d" % t) for t in range(NT)]
-        for t in range(NT):
-            cols = slice(P * t, P * (t + 1))
-            product(d_ps[t][:], w2_codes[:, cols], w2_scales[:, cols], xw_two[:], xs_two[:])
+        d_win = []
 
-        xs_offs = gather("xs_offs", U8, xs_win[:], offs_l)
-        xw_offs = gather("xw_offs", U32, xw_win[:].bitcast(U32), offs_l)
-        ds_picked = gather("ds_picked", U8, ds_win[:], k1_l)
+        def make_d(t):
+            d_win.append(sb("d_win%d" % t, [P, S], F32, "w1_raw1" if t == 1 else None))
+            d_ps = bank(t, "d_ps%d" % t)
+            product(d_ps[:], w2_codes[:, block(t)], w2_scales[:, block(t)], xw_two[:], xs_two[:])
+            nc.scalar.copy(d_win[t][:], d_ps[:])
+
+        make_d(0)
+
+        ds_picked = gather("ds_picked", U8, ds_win[:], k1_l, "w2_raw1")
         ds_dealt = sb("ds_dealt", [P, H], U8)
         nc.vector.tensor_copy(ds_dealt[:].rearrange("p (t q i) -> p q t i", t=4, i=16), ds_picked[:].rearrange("p (q i t) -> p q t i", t=4, i=16))
-        for o in range(2):
+        for odd in range(2):
             for e in range(2):
-                nc.sync.dma_start(ds_plane[2 * o + e : P : 32, :].bitcast(I32), ds_dealt[16 * o + e : P : 32, :].bitcast(I32))
+                nc.sync.dma_start(ds_plane[2 * odd + e : P : 32, :].bitcast(I32), ds_dealt[16 * odd + e : P : 32, :].bitcast(I32))
 
-        nc.scalar.copy(d_win[0][:, :S], d_ps[0][:])
         w1_bf = cast_weight("w1", w1_raw)
-        for t in range(1, NT):
-            nc.scalar.copy(d_win[t][:, :S], d_ps[t][:])
-        w1_codes, w1_scales = quantize("w1", w1_bf)
-        y_ps = [bank(4 + t, "y_ps%d" % t) for t in range(NT)]
-        for t in range(NT):
-            cols = slice(P * t, P * (t + 1))
-            product(y_ps[t][:], w1_codes[:, cols], w1_scales[:, cols], xw_offs[:], xs_offs[:])
-        y_win = [sb("y_win%d" % t, [P, S], F32) for t in range(NT)]
-        y_own = [sb("y_own%d" % t, [P, S], F32) for t in range(NT)]
-        for t in range(NT):
-            nc.scalar.activation(y_win[t][:], y_ps[t][:], ACT.Copy, scale=gs_t[:, t : t + 1])
-            nc.scalar.activation(y_own[t][:], y_ps[t][:], ACT.Copy, scale=gs_t[:, t : t + 1])
+        for t in range(1, TILES):
+            make_d(t)
+        w1_codes, w1_scales = quantize_weight("w1", w1_bf)
+        y_win = [sb("y_win%d" % t, [P, WINDOW], F32, "w1_bf" if t == 1 else None) for t in range(TILES)]
+        for t in range(TILES):
+            y_ps = bank(t, "y_ps%d" % t)
+            product(y_ps[:], w1_codes[:, block(t)], w1_scales[:, block(t)], xw_offs[:], xs_offs[:])
+            nc.scalar.activation(y_win[t][:, :S], y_ps[:], ACT.Copy, scale=gs_t[:, t : t + 1])
 
-        ds_ps = [bank(b, "ds_ps%d" % b) for b in range(4)]
-        d_nb = [h_win[t][:, S:] for t in range(NT)]
-        for t in range(NT):
-            nc.vector.tensor_copy(d_nb[t], d_win[t][:].indirect(n2_l[:]))
-        for t in range(NT):
-            for b in range(4):
-                add_transpose(ds_ps[b][:, P * t : P * (t + 1)], d_win[t][:, P * b : P * (b + 1)], t == 0, False)
-            for b in range(4):
-                add_transpose(ds_ps[b][:, P * t : P * (t + 1)], d_nb[t][:, P * b : P * (b + 1)], False, t == NT - 1)
-        gate = [sb("gate%d" % b, [P, K], F32) for b in range(4)]
-        for b in range(4):
-            nc.scalar.activation(gate[b][:].rearrange("p (a t c) -> p a t c", t=4, c=4), ds_ps[b][:].rearrange("p (t a c) -> p a t c", t=4, c=4), ACT.Sigmoid)
-        warm2 = sb("warm2", [P, 1], F32)
-        nc.scalar.activation(warm2[:], gate[3][:, 0:1], ACT.Abs_reciprocal_sqrt, bias=1.0)
+        def add_neighbours(sums, window, picked, offsets, pieces):
+            n = S // pieces
+            for t in range(TILES):
+                for i in range(pieces):
+                    nc.vector.tensor_copy(picked[t][:, n * i : n * (i + 1)], window[t][:].indirect(offsets[:, n * i // 16 : n * (i + 1) // 16]))
+            for t in range(TILES):
+                for b in range(BLOCKS):
+                    add_transpose(sums[b][:, block(t)], window[t][:, block(b)], t == 0, False)
+            for t in range(TILES):
+                for b in range(BLOCKS):
+                    add_transpose(sums[b][:, block(t)], picked[t][:, block(b)], False, t == TILES - 1)
 
-        ys_ps = [bank(4 + b, "ys_ps%d" % b) for b in range(4)]
-        for half in range(2):
-            lo, hi = 2 * P * half, 2 * P * (half + 1)
-            for t in range(NT):
-                y_sum = sb("y_sum%d_%d" % (half, t), [P, 2 * P], F32)
-                nc.vector.tensor_tensor(y_sum[:], y_win[t][:].indirect(n1_l[:, lo // 16 : hi // 16]), y_own[t][:, lo:hi], ALU.add)
-                for i in range(2):
-                    nc.tensor.transpose(ys_ps[2 * half + i][:, P * t : P * (t + 1)], y_sum[:, P * i : P * (i + 1)], ident[:])
+        def by_tile(ap):
+            return ap.rearrange("p (t a c) -> p a t c", t=4, c=4)
 
-        z_rows = [sb("z_rows%d" % b, [P, K], BF16) for b in range(4)]
-        z_bf = [sb("z_bf%d" % b, [P, 4 * P], BF16) for b in range(4)]
-        z_codes = [sb("z_codes%d" % b, [P, P], U32) for b in range(4)]
-        z_scales = [sb("z_scales%d" % b, [P, P], U8) for b in range(4)]
-        h_ps = [bank(t, "h_ps%d" % t) for t in range(NT)]
+        def by_row(ap):
+            return ap.rearrange("p (a t c) -> p a t c", t=4, c=4)
 
-        for b in range(4):
-            nc.vector.tensor_tensor(
-                z_rows[b][:].rearrange("p (a t c) -> p a t c", t=4, c=4),
-                ys_ps[b][:].rearrange("p (t a c) -> p a t c", t=4, c=4),
-                gate[b][:].rearrange("p (a t c) -> p a t c", t=4, c=4),
-                ALU.mult,
-            )
-            pairs = bank(4 + b, "pairs%d" % b)
+        d_sums = [bank(4 + b, "d_sums%d" % b) for b in range(BLOCKS)]
+        add_neighbours(d_sums, d_win, [y_win[t][:, S:] for t in range(TILES)], n2_l, 2)
+        gate = [sb("gate%d" % b, [P, K], F32) for b in range(BLOCKS)]
+        for b in range(BLOCKS):
+            nc.scalar.activation(by_row(gate[b][:]), by_tile(d_sums[b][:]), ACT.Sigmoid)
+        warm_root = sb("warm_root", [P, 1], F32)
+        nc.scalar.activation(warm_root[:], gate[BLOCKS - 1][:, 0:1], ACT.Abs_reciprocal_sqrt, bias=1.0)
+
+        y_sums = [bank(b, "y_sums%d" % b) for b in range(BLOCKS)]
+        add_neighbours(y_sums, y_win, [h_win[t][:, S:] for t in range(TILES)], n1_l, 1)
+        dw_picked = gather("dw_picked", U32, dw_win[:].bitcast(U32), k1_l, "y_win%d" % (TILES - 1))
+
+        z_rows = [sb("z_rows%d" % b, [P, K], BF16) for b in range(BLOCKS)]
+        z_bf = [sb("z_bf%d" % b, [P, 4 * P], BF16) for b in range(BLOCKS)]
+        z_codes = [sb("z_codes%d" % b, [P, P], U32) for b in range(BLOCKS)]
+        z_scales = [sb("z_scales%d" % b, [P, P], U8) for b in range(BLOCKS)]
+        h_ps = [bank(4 + t, "h_ps%d" % t) for t in range(TILES)]
+
+        for b in range(BLOCKS):
+            nc.vector.tensor_tensor(by_row(z_rows[b][:]), by_tile(y_sums[b][:]), by_row(gate[b][:]), ALU.mult)
+            pairs = bank(b, "pairs%d" % b)
             words = z_rows[b][:].bitcast(F32)
             for u in range(2):
-                nc.tensor.transpose(pairs[:, P * u : P * (u + 1)], words[:, u : 2 * P : 2], ident[:])
+                nc.tensor.transpose(pairs[:, block(u)], words[:, u : 2 * P : 2], ident[:])
             nc.scalar.copy(
                 z_bf[b][:].bitcast(F32).rearrange("p (j u) -> p j u", u=2),
                 pairs[:, : 2 * P].rearrange("p (u j) -> p j u", u=2),
             )
 
-        dw_picked = gather("dw_picked", U32, dw_win[:].bitcast(U32), k1_l)
-        dw_dealt = sb("dw_dealt", [P, H], U32)
-        nc.vector.tensor_copy(dw_dealt[:].rearrange("p (t q i) -> p q t i", t=4, i=4), dw_picked[:].rearrange("p (q i t) -> p q t i", t=4, i=4))
-
-        for b in range(4):
+        def quantize_z(b):
             nc.vector.quantize_mx(z_codes[b][:].bitcast(FP8X4), z_scales[b][:], z_bf[b][:])
-            for t in range(NT):
-                cols = slice(P * t, P * (t + 1))
-                product(h_ps[t][:, P * b : P * (b + 1)], dw_dealt[:, cols], ds_plane[:, cols], z_codes[b][:], z_scales[b][:])
-            if b == 2:
-                for t in range(NT):
-                    nc.scalar.activation(h_win[t][:, :FIRST], h_ps[t][:, :FIRST], ACT.Copy, scale=ALPHA)
-        for t in range(NT):
-            nc.scalar.activation(h_win[t][:, FIRST:S], h_ps[t][:, FIRST:], ACT.Copy, scale=ALPHA)
+
+        quantize_z(0)
+        quantize_z(1)
+        dw_dealt = sb("dw_dealt", [P, H], U32, "z_bf1")
+        nc.vector.tensor_copy(dw_dealt[:].rearrange("p (t q i) -> p q t i", t=4, i=4), dw_picked[:].rearrange("p (q i t) -> p q t i", t=4, i=4))
+        quantize_z(2)
+        quantize_z(3)
+        for t in range(TILES):
+            for b in range(BLOCKS):
+                product(h_ps[t][:, block(b)], dw_dealt[:, block(t)], ds_plane[:, block(t)], z_codes[b][:], z_scales[b][:])
+            nc.scalar.activation(h_win[t][:, :S], h_ps[t][:], ACT.Copy, scale=WINDOW_FACTOR)
 
         out_rows = out.rearrange("(p t) j -> t p j", t=4)
-        pieces = [(0, 0, S), (1, 0, S), (2, 0, S), (3, 0, S // 2), (3, S // 2, S)]
-        tiles = {}
+        made = {}
 
-        def piece_tile(name, n):
-            t, lo, hi = pieces[n]
-            tiles[name, n] = sb("%s%d" % (name, n), [P, hi - lo], F32)
-            return tiles[name, n]
+        def new(name, t, slot=None):
+            made[name, t] = sb("%s%d" % (name, t), [P, S], F32, slot)
+            return made[name, t][:]
 
-        def add_both(n, name, slot, first, second):
-            t, lo, hi = pieces[n]
-            acc = bank(BANKS[n][slot], "%s%d" % (name, n))
-            for c in range(0, hi - lo, P):
-                add_transpose(acc[:, c : c + P], first[:, c : c + P], True, second is None)
-                if second is not None:
-                    add_transpose(acc[:, c : c + P], second[:, c : c + P], False, True)
-            return acc[:, : hi - lo]
+        def got(name, t):
+            return made[name, t][:]
 
-        def fetch_a(n):
-            t, lo, hi = pieces[n]
-            nc.vector.tensor_copy(piece_tile("pa", n)[:], h_win[t][:].indirect(n3_l[:, lo // 16 : hi // 16]))
+        def square(name, t, src, scale):
+            nc.scalar.activation(new(name, t, "%s_slot%d" % (name, t % 2)), src, ACT.Square, scale=scale)
 
-        def fetch_b(n):
-            t, lo, hi = pieces[n]
-            nc.vector.tensor_tensor(piece_tile("diff", n)[:], h_win[t][:].indirect(n4_l[:, lo // 16 : hi // 16]), tiles["pa", n][:], ALU.subtract)
-            diff = add_both(n, "diff_ps", 0, tiles["diff", n], None)
-            nc.scalar.activation(piece_tile("diff_sq", n)[:], diff, ACT.Square, scale=HS / (ALPHA * math.sqrt(2.0)))
+        def transposed_sum(t, which, first, second):
+            acc = bank(NORM_BANKS[t][which], "norm_ps%d_%d" % (t, which))
+            for b in range(BLOCKS):
+                add_transpose(acc[:, block(b)], first[:, block(b)], True, False)
+                add_transpose(acc[:, block(b)], second[:, block(b)], False, True)
+            return acc[:]
 
-        def sum_pair(n):
-            nc.vector.scalar_tensor_tensor(piece_tile("both", n)[:], tiles["pa", n][:], 2.0, tiles["diff", n][:], ALU.mult, ALU.add)
+        def less_h(name, t, factor):
+            nc.vector.scalar_tensor_tensor(new(name, t), got("both", t), factor, h_ps[t][:], ALU.mult, ALU.subtract)
 
-        def centre(n):
-            t, lo, hi = pieces[n]
-            top = piece_tile("top", n)
-            nc.vector.scalar_tensor_tensor(top[:], tiles["both", n][:], 1.0 / (2.2 * ALPHA), h_ps[t][:, lo:hi], ALU.mult, ALU.subtract)
-            mean = add_both(n, "mean_ps", 1, tiles["both", n], top)
-            nc.scalar.activation(piece_tile("mean_sq", n)[:], mean, ACT.Square, scale=HS * 0.3125 * math.sqrt(2.0))
-            var = add_both(n, "var_ps", 2, tiles["diff_sq", n], tiles["mean_sq", n])
-            nc.scalar.activation(piece_tile("inv", n)[:], var, ACT.Abs_reciprocal_sqrt, bias=0.25)
+        def inverse_root(t, variance):
+            nc.scalar.activation(new("inv", t), variance, ACT.Abs_reciprocal_sqrt, bias=0.25)
 
-        def finish(n):
-            t, lo, hi = pieces[n]
-            res = piece_tile("res", n)
-            nc.vector.scalar_tensor_tensor(res[:], tiles["top", n][:], -HS * 0.6875, tiles["inv", n][:], ALU.mult, ALU.mult)
-            nc.sync.dma_start(out_rows[t][:, lo:hi], res[:])
+        def fetch_first(t):
+            window = h_win[t][:].indirect(n3_l[:])
+            if t == LAST:
+                nc.vector.tensor_copy(new("pa", t), window)
+            else:
+                nc.vector.tensor_scalar(new("neg_pa", t), window, -1.0, 0.0, ALU.mult, ALU.add)
 
-        last = len(pieces) - 1
-        fetch_a(0)
-        fetch_b(0)
-        for n in range(last):
-            fetch_a(n + 1)
-            sum_pair(n)
-            fetch_b(n + 1)
-            centre(n)
+        def fetch_second(t):
+            window = h_win[t][:].indirect(n4_l[:])
+            if t == LAST:
+                nc.vector.tensor_tensor(new("diff", t), window, got("pa", t), ALU.subtract)
+                square("diff_sq", t, got("diff", t), DIFF_SCALE)
+            else:
+                nc.vector.tensor_tensor(new("both", t), window, got("neg_pa", t), ALU.subtract)
+                nc.scalar.activation(new("neg_2pa", t, "neg_2pa"), got("neg_pa", t), ACT.Copy, scale=2.0)
+                square("diff_sq", t, transposed_sum(t, 0, got("both", t), got("neg_2pa", t)), DIFF_SCALE)
+
+        def centre(t):
+            if t == LAST:
+                nc.vector.scalar_tensor_tensor(new("both", t), got("pa", t), 2.0, got("diff", t), ALU.mult, ALU.add)
+                less_h("mean", t, MEAN_FACTOR)
+                square("mean_sq", t, got("mean", t), MEAN_SCALE)
+                less_h("top", t, TOP_FACTOR)
+            else:
+                less_h("top", t, TOP_FACTOR)
+                square("mean_sq", t, transposed_sum(t, 1, got("top", t), got("both", t)), MEAN_SCALE)
+
+        def spread(t):
+            if t == LAST:
+                nc.vector.tensor_tensor(new("var", t), got("diff_sq", t), got("mean_sq", t), ALU.add)
+                inverse_root(t, got("var", t))
+            else:
+                inverse_root(t, transposed_sum(t, 2, got("diff_sq", t), got("mean_sq", t)))
+
+        def finish(t):
+            nc.vector.scalar_tensor_tensor(new("res", t), got("top", t), OUT_FACTOR, got("inv", t), ALU.mult, ALU.mult)
+            nc.sync.dma_start(out_rows[t], got("res", t))
+
+        fetch_first(0)
+        for t in range(TILES):
+            fetch_second(t)
+            if t < LAST:
+                fetch_first(t + 1)
+            if t > 0:
+                spread(t - 1)
+            centre(t)
         finish(0)
-        sum_pair(last)
-        finish(1)
-        centre(last)
-        for n in range(2, last + 1):
-            finish(n)
+        spread(LAST)
+        for t in range(1, TILES):
+            finish(t)

import math
from contextlib import ExitStack

import concourse.mybir as mybir
from concourse.masks import make_identity

K, T, S, H, G = 512, 1024, 512, 512, 2048
FLOPS = 3 * 2 * K * H * S

F32 = mybir.dt.float32
BF16 = mybir.dt.bfloat16
I32 = mybir.dt.int32
U32 = mybir.dt.uint32
U16 = mybir.dt.uint16
U8 = mybir.dt.uint8
FP8X4 = mybir.dt.float8_e4m3fn_x4
ALU = mybir.AluOpType
ACT = mybir.ActivationFunctionType

P = 128
TILES = 4
BLOCKS = S // P
WINDOW = 2 * S
HALF = H // 2

H_FACTOR = 0.0625
WINDOW_FACTOR = 0.6 - 1.0 / 2.2
TOP_FACTOR = 1.0 / (2.2 * WINDOW_FACTOR)
MEAN_FACTOR = 0.6 / WINDOW_FACTOR
DIFF_SCALE = H_FACTOR / (WINDOW_FACTOR * math.sqrt(2.0))
MEAN_SCALE = H_FACTOR * 0.3125 * math.sqrt(2.0)
OUT_FACTOR = -H_FACTOR * 0.6875

LAST = TILES - 1
NORM_BANKS = [(0, 1, 2), (3, 0, 1), (4, 3, 2)]


def tile_picked_twqtriebstd_none_p_kernel(
    tc, x_words, x_scales, w1, w2, gs, d_words, d_scales, offs, two, n1, n2, k1, n3, n4, out
):
    nc = tc.nc
    with ExitStack() as ctx:
        lists = ctx.enter_context(tc.tile_pool(name="lists", bufs=1))
        keep = ctx.enter_context(tc.tile_pool(name="keep", bufs=1))
        psum = ctx.enter_context(tc.psum_pool(name="psum", bufs=1))

        def sb(name, shape, dtype, slot=None):
            return keep.tile(shape, dtype, name=name, tag=slot or name, align_bytes=64)

        def bank(index, name):
            return psum.tile([P, 512], F32, name=name, tag="bank%d" % index)

        def block(i):
            return slice(P * i, P * (i + 1))

        def load_list(name, src):
            tile = lists.tile([P, S // 16], U16, name=name)
            nc.sync.dma_start(tile[:], src)
            return tile

        def load_half(name, w, half):
            raw = sb("%s_raw%d" % (name, half), [P, 4, HALF], F32)
            nc.sync.dma_start(raw[:], w.rearrange("(p j) c -> p j c", j=4)[:, :, HALF * half : HALF * (half + 1)])
            return raw

        def add_transpose(dst, src, start, stop):
            nc.tensor.matmul(dst, src, ident[:], start=start, stop=stop, is_transpose=True)

        def gather(name, dtype, window, offsets, slot=None):
            picked = sb(name, [P, S], dtype, slot)
            nc.vector.tensor_copy(picked[:], window.indirect(offsets[:]))
            return picked

        def product(dst, lhs, lhs_scale, rhs, rhs_scale):
            nc.tensor.matmul_mx(dst, lhsT=lhs.bitcast(FP8X4), lhsT_scale=lhs_scale, rhs=rhs.bitcast(FP8X4), rhs_scale=rhs_scale, start=True, stop=True)

        xs_win = sb("xs_win", [P, T], U8)
        ds_win = sb("ds_win", [P, G], U8)
        ds_plane = sb("ds_plane", [P, H], U8)
        nc.gpsimd.memset(xs_win[:].bitcast(I32), 0)
        nc.vector.memset(ds_win[:].bitcast(I32), 0)
        warm = sb("warm", [P, 2], F32)
        nc.vector.memset(warm[:, 0:1], 0.0)
        nc.scalar.activation(warm[:, 1:2], warm[:, 0:1], ACT.Sigmoid)

        two_l = load_list("two_l", two)
        offs_l = load_list("offs_l", offs)
        k1_l = load_list("k1_l", k1)
        xw_win = sb("xw_win", [P, T], I32)
        nc.sync.dma_start(xw_win[:], x_words[0].rearrange("p n t -> p (n t)").bitcast(I32))
        for r in range(4):
            nc.sync.dma_start(xs_win[r:P:32, :].bitcast(I32), x_scales[0, r:16:4, :].bitcast(I32))
        w2_raw = [load_half("w2", w2, 0), load_half("w2", w2, 1)]
        for e in range(2):
            nc.sync.dma_start(ds_win[e:P:16, :].bitcast(I32), d_scales[0, e:16:2, :].bitcast(I32))
        n2_l = load_list("n2_l", n2)
        w1_raw = [load_half("w1", w1, 0), load_half("w1", w1, 1)]
        gs_t = sb("gs_t", [P, TILES], F32)
        with nc.allow_non_contiguous_dma(reason="one gain for each partition and tile"):
            for c in range(4):
                nc.sync.dma_start(gs_t[c:P:4, :], gs.rearrange("(a t c) o -> c a (t o)", t=4, c=4)[c])
        n1_l = load_list("n1_l", n1)
        dw_win = sb("dw_win", [P, G], I32)
        nc.sync.dma_start(dw_win[:], d_words[0].rearrange("p n t -> p (n t)").bitcast(I32))
        n3_l = load_list("n3_l", n3)
        n4_l = load_list("n4_l", n4)

        ident = sb("ident", [P, P], F32)
        make_identity(nc, ident[:])
        h_win = [sb("h_win%d" % t, [P, WINDOW], F32) for t in range(TILES)]
        nc.vector.memset(ds_plane[:].bitcast(I32), 0)

        xs_two = gather("xs_two", U8, xs_win[:], two_l)
        xw_two = gather("xw_two", U32, xw_win[:].bitcast(U32), two_l)
        xw_offs = gather("xw_offs", U32, xw_win[:].bitcast(U32), offs_l)
        xs_offs = gather("xs_offs", U8, xs_win[:], offs_l)

        def cast_weight(name, halves):
            grouped = sb(name + "_bf", [P, 4 * H], BF16)
            dst = grouped[:].rearrange("p (t a c j) -> p t a c j", t=4, c=4, j=4)
            for half in range(2):
                nc.scalar.copy(dst[:, :, 16 * half : 16 * (half + 1)], halves[half][:].rearrange("p j (a t c) -> p t a c j", t=4, c=4))
            return grouped

        def quantize_weight(name, grouped):
            codes = sb(name + "_codes", [P, H], U32)
            scales = sb(name + "_scales", [P, H], U8)
            nc.vector.quantize_mx(codes[:].bitcast(FP8X4), scales[:], grouped[:])
            return codes, scales

        w2_codes, w2_scales = quantize_weight("w2", cast_weight("w2", w2_raw))

        d_win = []

        def make_d(t):
            d_win.append(sb("d_win%d" % t, [P, S], F32, "w1_raw1" if t == 1 else None))
            d_ps = bank(t, "d_ps%d" % t)
            product(d_ps[:], w2_codes[:, block(t)], w2_scales[:, block(t)], xw_two[:], xs_two[:])
            nc.scalar.copy(d_win[t][:], d_ps[:])

        make_d(0)

        ds_picked = gather("ds_picked", U8, ds_win[:], k1_l, "w2_raw1")
        ds_dealt = sb("ds_dealt", [P, H], U8)
        nc.vector.tensor_copy(ds_dealt[:].rearrange("p (t q i) -> p q t i", t=4, i=16), ds_picked[:].rearrange("p (q i t) -> p q t i", t=4, i=16))
        for odd in range(2):
            for e in range(2):
                nc.sync.dma_start(ds_plane[2 * odd + e : P : 32, :].bitcast(I32), ds_dealt[16 * odd + e : P : 32, :].bitcast(I32))

        w1_bf = cast_weight("w1", w1_raw)
        for t in range(1, TILES):
            make_d(t)
        w1_codes, w1_scales = quantize_weight("w1", w1_bf)
        y_win = [sb("y_win%d" % t, [P, WINDOW], F32, "w1_bf" if t == 1 else None) for t in range(TILES)]
        for t in range(TILES):
            y_ps = bank(t, "y_ps%d" % t)
            product(y_ps[:], w1_codes[:, block(t)], w1_scales[:, block(t)], xw_offs[:], xs_offs[:])
            nc.scalar.activation(y_win[t][:, :S], y_ps[:], ACT.Copy, scale=gs_t[:, t : t + 1])

        def add_neighbours(sums, window, picked, offsets, pieces):
            n = S // pieces
            for t in range(TILES):
                for i in range(pieces):
                    nc.vector.tensor_copy(picked[t][:, n * i : n * (i + 1)], window[t][:].indirect(offsets[:, n * i // 16 : n * (i + 1) // 16]))
            for t in range(TILES):
                for b in range(BLOCKS):
                    add_transpose(sums[b][:, block(t)], window[t][:, block(b)], t == 0, False)
            for t in range(TILES):
                for b in range(BLOCKS):
                    add_transpose(sums[b][:, block(t)], picked[t][:, block(b)], False, t == TILES - 1)

        def by_tile(ap):
            return ap.rearrange("p (t a c) -> p a t c", t=4, c=4)

        def by_row(ap):
            return ap.rearrange("p (a t c) -> p a t c", t=4, c=4)

        d_sums = [bank(4 + b, "d_sums%d" % b) for b in range(BLOCKS)]
        add_neighbours(d_sums, d_win, [y_win[t][:, S:] for t in range(TILES)], n2_l, 2)
        gate = [sb("gate%d" % b, [P, K], F32) for b in range(BLOCKS)]
        for b in range(BLOCKS):
            nc.scalar.activation(by_row(gate[b][:]), by_tile(d_sums[b][:]), ACT.Sigmoid)
        warm_root = sb("warm_root", [P, 1], F32)
        nc.scalar.activation(warm_root[:], gate[BLOCKS - 1][:, 0:1], ACT.Abs_reciprocal_sqrt, bias=1.0)

        y_sums = [bank(b, "y_sums%d" % b) for b in range(BLOCKS)]
        add_neighbours(y_sums, y_win, [h_win[t][:, S:] for t in range(TILES)], n1_l, 1)
        dw_picked = gather("dw_picked", U32, dw_win[:].bitcast(U32), k1_l, "y_win%d" % (TILES - 1))

        z_rows = [sb("z_rows%d" % b, [P, K], BF16) for b in range(BLOCKS)]
        z_bf = [sb("z_bf%d" % b, [P, 4 * P], BF16) for b in range(BLOCKS)]
        z_codes = [sb("z_codes%d" % b, [P, P], U32) for b in range(BLOCKS)]
        z_scales = [sb("z_scales%d" % b, [P, P], U8) for b in range(BLOCKS)]
        h_ps = [bank(4 + t, "h_ps%d" % t) for t in range(TILES)]

        for b in range(BLOCKS):
            nc.vector.tensor_tensor(by_row(z_rows[b][:]), by_tile(y_sums[b][:]), by_row(gate[b][:]), ALU.mult)
            pairs = bank(b, "pairs%d" % b)
            words = z_rows[b][:].bitcast(F32)
            for u in range(2):
                nc.tensor.transpose(pairs[:, block(u)], words[:, u : 2 * P : 2], ident[:])
            nc.scalar.copy(
                z_bf[b][:].bitcast(F32).rearrange("p (j u) -> p j u", u=2),
                pairs[:, : 2 * P].rearrange("p (u j) -> p j u", u=2),
            )

        def quantize_z(b):
            nc.vector.quantize_mx(z_codes[b][:].bitcast(FP8X4), z_scales[b][:], z_bf[b][:])

        quantize_z(0)
        quantize_z(1)
        dw_dealt = sb("dw_dealt", [P, H], U32, "z_bf1")
        nc.vector.tensor_copy(dw_dealt[:].rearrange("p (t q i) -> p q t i", t=4, i=4), dw_picked[:].rearrange("p (q i t) -> p q t i", t=4, i=4))
        quantize_z(2)
        quantize_z(3)
        for t in range(TILES):
            for b in range(BLOCKS):
                product(h_ps[t][:, block(b)], dw_dealt[:, block(t)], ds_plane[:, block(t)], z_codes[b][:], z_scales[b][:])
            nc.scalar.activation(h_win[t][:, :S], h_ps[t][:], ACT.Copy, scale=WINDOW_FACTOR)

        out_rows = out.rearrange("(p t) j -> t p j", t=4)
        made = {}

        def new(name, t, slot=None):
            made[name, t] = sb("%s%d" % (name, t), [P, S], F32, slot)
            return made[name, t][:]

        def got(name, t):
            return made[name, t][:]

        def square(name, t, src, scale):
            nc.scalar.activation(new(name, t, "%s_slot%d" % (name, t % 2)), src, ACT.Square, scale=scale)

        def transposed_sum(t, which, first, second):
            acc = bank(NORM_BANKS[t][which], "norm_ps%d_%d" % (t, which))
            for b in range(BLOCKS):
                add_transpose(acc[:, block(b)], first[:, block(b)], True, False)
                add_transpose(acc[:, block(b)], second[:, block(b)], False, True)
            return acc[:]

        def less_h(name, t, factor):
            nc.vector.scalar_tensor_tensor(new(name, t), got("both", t), factor, h_ps[t][:], ALU.mult, ALU.subtract)

        def inverse_root(t, variance):
            nc.scalar.activation(new("inv", t), variance, ACT.Abs_reciprocal_sqrt, bias=0.25)

        def fetch_first(t):
            window = h_win[t][:].indirect(n3_l[:])
            if t == LAST:
                nc.vector.tensor_copy(new("pa", t), window)
            else:
                nc.vector.tensor_scalar(new("neg_pa", t), window, -1.0, 0.0, ALU.mult, ALU.add)

        def fetch_second(t):
            window = h_win[t][:].indirect(n4_l[:])
            if t == LAST:
                nc.vector.tensor_tensor(new("diff", t), window, got("pa", t), ALU.subtract)
                square("diff_sq", t, got("diff", t), DIFF_SCALE)
            else:
                nc.vector.tensor_tensor(new("both", t), window, got("neg_pa", t), ALU.subtract)
                nc.scalar.activation(new("neg_2pa", t, "neg_2pa"), got("neg_pa", t), ACT.Copy, scale=2.0)
                square("diff_sq", t, transposed_sum(t, 0, got("both", t), got("neg_2pa", t)), DIFF_SCALE)

        def centre(t):
            if t == LAST:
                nc.vector.scalar_tensor_tensor(new("both", t), got("pa", t), 2.0, got("diff", t), ALU.mult, ALU.add)
                less_h("mean", t, MEAN_FACTOR)
                square("mean_sq", t, got("mean", t), MEAN_SCALE)
                less_h("top", t, TOP_FACTOR)
            else:
                less_h("top", t, TOP_FACTOR)
                square("mean_sq", t, transposed_sum(t, 1, got("top", t), got("both", t)), MEAN_SCALE)

        def spread(t):
            if t == LAST:
                nc.vector.tensor_tensor(new("var", t), got("diff_sq", t), got("mean_sq", t), ALU.add)
                inverse_root(t, got("var", t))
            else:
                inverse_root(t, transposed_sum(t, 2, got("diff_sq", t), got("mean_sq", t)))

        def finish(t):
            nc.vector.scalar_tensor_tensor(new("res", t), got("top", t), OUT_FACTOR, got("inv", t), ALU.mult, ALU.mult)
            nc.sync.dma_start(out_rows[t], got("res", t))

        fetch_first(0)
        for t in range(TILES):
            fetch_second(t)
            if t < LAST:
                fetch_first(t + 1)
            if t > 0:
                spread(t - 1)
            centre(t)
        finish(0)
        spread(LAST)
        for t in range(1, TILES):
            finish(t)
